import numpy as np
import ml_dtypes


def mxq(x, axis, fmt="e4m3"):
    dtype, down = {"e4m3": (ml_dtypes.float8_e4m3fn, 7), "e5m2": (ml_dtypes.float8_e5m2, 14)}[fmt]
    v = np.moveaxis(np.asarray(x, np.float32).astype(ml_dtypes.bfloat16).astype(np.float64), axis, -1)
    blocks = v.reshape(v.shape[:-1] + (-1, 32))
    amax = np.abs(blocks).max(-1, keepdims=True)
    byte = np.maximum(np.where(amax > 0, np.frexp(amax)[1] - 1 + 127, 0) - down, 1)
    scale = np.exp2(byte - 127.0)
    codes = (blocks / scale).astype(np.float32).astype(dtype).astype(np.float64)
    return np.moveaxis((codes * scale).reshape(v.shape), -1, axis)


WIDE = False


def mx_kscale(k):
    if not WIDE:
        return np.ones(k)
    levels = np.array([10, -10, 5, -5, 0])
    if k % 512:
        return np.exp2(np.random.permutation(np.resize(levels, k // 32))).repeat(32)
    a = np.empty((k // 512, 16))
    for p in range(k // 512):
        a[p, :8] = np.random.permutation(np.resize(levels, 8))
        for g in range(8):
            far = levels[np.abs(levels - a[p, g]) >= 10]
            a[p, g + 8] = far[np.random.randint(len(far))]
    return np.exp2(a.ravel()).repeat(32)


def f64(x):
    return np.asarray(x).astype(np.float64)


def striped8(idx):
    return np.asarray(idx).reshape(8, -1, 16).transpose(0, 2, 1).reshape(128, -1).astype(np.uint16)


def unstriped8(offs):
    return offs.reshape(8, 16, -1).transpose(0, 2, 1).reshape(8, -1).astype(np.int64)


def pick8(x, idx, run):
    r = np.arange(len(x))
    return x[r[:, None], idx[r % (8 * run) // run]]


E2M1 = np.array([0.0, 0.5, 1.0, 1.5, 2.0, 3.0, 4.0, 6.0, -0.0, -0.5, -1.0, -1.5, -2.0, -3.0, -4.0, -6.0])


def pack_weight(w, fmt):
    k, n = w.shape
    w = f64(np.asarray(w, np.float32).astype(ml_dtypes.bfloat16)).reshape(k // 32, 32, n)
    amax = np.abs(w).max(1)
    if fmt == "e4m3":
        byte = np.frexp(amax)[1] - 1 + 127 - 7
    else:
        mant, ex = np.frexp(amax / 6.0)
        byte = np.where(mant > 0.5, ex, ex - 1) + 127
    byte = np.clip(np.where(amax > 0, byte, 1), 1, 254)
    scaled = (w * np.exp2(127.0 - byte)[:, None, :]).reshape(k, n).astype(np.float32)
    by_word = np.ascontiguousarray(scaled.reshape(k // 512, 128, 4, n).transpose(0, 1, 3, 2))
    if fmt == "e4m3":
        words = by_word.astype(ml_dtypes.float8_e4m3fn).view(np.uint8)
    else:
        c = by_word.astype(ml_dtypes.float4_e2m1fn).view(np.uint8) & 0xF
        words = (c[..., 0::2] | (c[..., 1::2] << 4)).reshape(k // 512, 128, 2 * n)
    return np.ascontiguousarray(words), np.ascontiguousarray(byte.astype(np.uint8).reshape(k // 512, 16, n))


def unpack_weight(words, scales, fmt):
    g, _, n = scales.shape
    words = np.ascontiguousarray(words).reshape(g, 128, n, -1)
    if fmt == "e4m3":
        vals = words.view(ml_dtypes.float8_e4m3fn).astype(np.float64)
    else:
        nib = np.empty((g, 128, n, 4), np.uint8)
        nib[..., 0::2] = words & 0xF
        nib[..., 1::2] = words >> 4
        vals = E2M1[nib]
    vals = vals * np.repeat(np.exp2(scales.astype(np.float64) - 127.0), 8, axis=1)[..., None]
    return vals.transpose(0, 1, 3, 2).reshape(g * 512, n)


D, V, Q, I = 512, 2048, 128, 512


def setup_inputs():
    n = np.random.standard_normal
    idx = np.stack([np.random.permutation(V)[:I] for _ in range(8)])
    idx2 = np.stack([np.random.permutation(V)[:I] for _ in range(8)])
    fd = mx_kscale(D)
    vocp = pack_weight(n((D, V)) / fd[:, None], "e2m1")
    return {
        "hid": (n((D, Q)) * 1.0 / np.sqrt(D) * fd[:, None]).astype(np.float32),
        "voc_words": vocp[0],
        "voc_scales": vocp[1],
        "stake": (np.random.uniform(0.5, 2.0, (Q, 1))).astype(np.float32),
        "dhid": (n((D, Q)) * 1.0 / np.sqrt(D) * fd[:, None]).astype(np.float32),
        "base": (0.5 * n((Q, V))).astype(np.float32),
        "offs": striped8(idx),
        "offs2": striped8(idx2),
    }


def reference(hid, voc_words, voc_scales, stake, dhid, base, offs, offs2):
    idx = unstriped8(offs)
    idx2 = unstriped8(offs2)
    vocu = unpack_weight(voc_words, voc_scales, "e2m1")
    hidq = mxq(f64(hid), 0, "e4m3")
    a = hidq.T @ vocu
    dhidq = mxq(f64(dhid), 0, "e4m3")
    ta = dhidq.T @ vocu
    m1 = np.max(a, axis=1, keepdims=True)
    p = np.exp(a - m1)
    z = np.sum(p, axis=1, keepdims=True)
    px = np.exp(pick8(a, idx, 16) - m1)
    px2 = np.exp(pick8(a, idx2, 16) - m1)
    ma = np.sum(px, axis=1, keepdims=True) / z
    mb = np.sum(px2, axis=1, keepdims=True) / z
    dmb = f64(stake) / (ma * mb * 16.0 + 1.0) * 16.0 * ma
    dma = f64(stake) / (ma * mb * 16.0 + 1.0) * 16.0 * mb
    dpx2 = dmb / z
    dpx = dma / z
    dz = dmb * np.sum(px2, axis=1, keepdims=True) / np.square(z) * (-1.0) - dma * np.sum(px, axis=1, keepdims=True) / np.square(z)
    xp = ta * p
    xz = np.sum(xp, axis=1, keepdims=True)
    xpx = pick8(ta, idx, 16) * px
    xpx2 = pick8(ta, idx2, 16) * px2
    xma = (np.sum(xpx, axis=1, keepdims=True) - xz * np.sum(px, axis=1, keepdims=True) / z) / z
    xmb = (np.sum(xpx2, axis=1, keepdims=True) - xz * np.sum(px2, axis=1, keepdims=True) / z) / z
    xdmb = (xma * mb + xmb * ma) * 16.0 * f64(stake) / np.square(ma * mb * 16.0 + 1.0) * (-1.0) * 16.0 * ma + xma * f64(stake) / (ma * mb * 16.0 + 1.0) * 16.0
    xdma = (xma * mb + xmb * ma) * 16.0 * f64(stake) / np.square(ma * mb * 16.0 + 1.0) * (-1.0) * 16.0 * mb + xmb * f64(stake) / (ma * mb * 16.0 + 1.0) * 16.0
    xdpx2 = (xdmb - xz * dmb / z) / z
    xdpx = (xdma - xz * dma / z) / z
    xdz = (xdmb * np.sum(px2, axis=1, keepdims=True) + np.sum(xpx2, axis=1, keepdims=True) * dmb - xz * z * 2.0 * dmb * np.sum(px2, axis=1, keepdims=True) / np.square(z)) / np.square(z) * (-1.0) - (xdma * np.sum(px, axis=1, keepdims=True) + np.sum(xpx, axis=1, keepdims=True) * dma - xz * z * 2.0 * dma * np.sum(px, axis=1, keepdims=True) / np.square(z)) / np.square(z)
    xe1 = xdpx2 * px2 + xpx2 * dpx2
    xs1 = np.zeros((Q, V))
    xs1[np.arange(Q)[:, None], idx2[np.arange(Q) % 128 // 16]] = xe1
    xe2 = xdpx * px + xpx * dpx
    xs2 = np.zeros((Q, V))
    xs2[np.arange(Q)[:, None], idx[np.arange(Q) % 128 // 16]] = xe2
    xda = xdz * p + xp * dz + xs1 + xs2
    y = xda * 512.0 + f64(base)
    return y

@@ -1,0 +1,258 @@
+from contextlib import ExitStack
+
+import concourse.mybir as mybir
+from concourse.masks import make_identity
+
+D, V, Q, NL = 512, 2048, 128, 512
+FLOPS = 2 * 2 * D * Q * V
+
+F32 = mybir.dt.float32
+BF16 = mybir.dt.bfloat16
+I32 = mybir.dt.int32
+U32 = mybir.dt.uint32
+U16 = mybir.dt.uint16
+U8 = mybir.dt.uint8
+FP8X4 = mybir.dt.float8_e4m3fn_x4
+FP4X4 = mybir.dt.float4_e2m1fn_x4
+ALU = mybir.AluOpType
+ACT = mybir.ActivationFunctionType
+AX = mybir.AxisListType
+
+P = 128
+BANK = 512
+NB = V // BANK
+
+
+def tile_attend_hvjointcover_heads_kernel(tc, hid, voc_words, voc_scales, stake, dhid, base, offs, offs2, out):
+    nc = tc.nc
+    mult, add, sub = ALU.mult, ALU.add, ALU.subtract
+    with ExitStack() as ctx:
+        lists = ctx.enter_context(tc.tile_pool(name="lists", bufs=1))
+        sb = ctx.enter_context(tc.tile_pool(name="sb", bufs=1))
+        ps = ctx.enter_context(tc.psum_pool(name="ps", bufs=1))
+
+        def cols(j):
+            return slice(j * BANK, (j + 1) * BANK)
+
+        vsc = sb.tile([P, V], U8, name="vsc", align_bytes=64)
+        nc.gpsimd.memset(vsc[:].bitcast(I32), 0)
+        zero = sb.tile([P, 1], F32, name="zero")
+        nc.vector.memset(zero[:], 0.0)
+        one = sb.tile([P, 1], F32, name="one")
+        nc.scalar.activation(out=one[:], in_=zero[:], func=ACT.Exp)
+
+        hraw = sb.tile([P, 4, Q], F32, name="hraw", tag="in0", align_bytes=64)
+        words = sb.tile([P, 2 * V], U8, name="words", tag="in2", align_bytes=64)
+        nc.sync.dma_start(out=hraw[:], in_=hid.rearrange("(p j) q -> p j q", j=4))
+        nc.sync.dma_start(out=words[:].bitcast(I32), in_=voc_words[0].bitcast(I32))
+        s32 = voc_scales[0].bitcast(I32)
+        for g in range(4):
+            nc.sync.dma_start(out=vsc[32 * g : 32 * g + 4, :].bitcast(I32), in_=s32[4 * g : 4 * g + 4, :])
+        draw = sb.tile([P, 4, Q], F32, name="draw", tag="in1", align_bytes=64)
+        nc.sync.dma_start(out=draw[:], in_=dhid.rearrange("(p j) q -> p j q", j=4))
+        o1 = lists.tile([P, NL // 16], U16, name="o1")
+        o2 = lists.tile([P, NL // 16], U16, name="o2")
+        nc.sync.dma_start(o1[:], offs)
+        nc.sync.dma_start(o2[:], offs2)
+
+        inp = sb.tile([P, 4], F32, name="inp")
+        nc.vector.memset(inp[:, 1:2], 16.0)
+        nc.vector.memset(inp[:, 2:3], -16.0)
+        nc.vector.memset(inp[:, 3:4], -1.0)
+        yy = sb.tile([P, 10], F32, name="yy")
+        nc.vector.memset(yy[:, 2:3], 0.125)
+        xs2 = sb.tile([P, V], F32, name="xs2")
+        nc.vector.memset(xs2[:], 0.0)
+        ident = sb.tile([P, P], F32, name="ident")
+        make_identity(nc, ident[:])
+
+        hg = sb.tile([P, Q, 4], BF16, name="hg", tag="hg", align_bytes=64)
+        dg = sb.tile([P, Q, 4], BF16, name="dg", tag="dg", align_bytes=64)
+        hq = sb.tile([P, Q], U32, name="hq", align_bytes=64)
+        dq = sb.tile([P, Q], U32, name="dq", align_bytes=64)
+        hs = sb.tile([P, Q], U8, name="hs", align_bytes=64)
+        ds = sb.tile([P, Q], U8, name="ds", align_bytes=64)
+        nc.vector.tensor_copy(out=hg[:], in_=hraw[:].rearrange("p j q -> p q j"))
+        nc.vector.quantize_mx(out=hq[:].bitcast(FP8X4), scales=hs[:], in_=hg[:].rearrange("p q j -> p (q j)"))
+        nc.scalar.copy(out=dg[:], in_=draw[:].rearrange("p j q -> p q j"))
+        nc.vector.quantize_mx(out=dq[:].bitcast(FP8X4), scales=ds[:], in_=dg[:].rearrange("p q j -> p (q j)"))
+
+        xs1 = sb.tile([P, V], F32, name="xs1", tag="dg", align_bytes=64)
+        nc.gpsimd.memset(xs1[:], 0.0)
+
+        def scores(codes, scales, tag):
+            banks = []
+            for j in range(NB):
+                b = ps.tile([P, BANK], F32, name=f"{tag}{j}", tag=f"{tag}{j}")
+                wj = words[:, 2 * j * BANK : 2 * (j + 1) * BANK]
+                nc.tensor.matmul_mx(out=b[:], lhsT=codes[:].bitcast(FP8X4), lhsT_scale=scales[:],
+                                    rhs=wj.bitcast(FP4X4), rhs_scale=vsc[:, cols(j)], start=True, stop=True)
+                banks.append(b)
+            return banks
+
+        pa = scores(hq, hs, "pa")
+        pt = scores(dq, ds, "pt")
+
+        stk = sb.tile([P, 1], F32, name="stk", tag="hg", align_bytes=64)
+        nc.sync.dma_start(out=stk[:], in_=stake)
+        bs01 = [sb.tile([P, BANK], F32, name=f"bs{j}", tag=f"in{j}", align_bytes=64) for j in range(2)]
+        bs23 = sb.tile([P, 2 * BANK], F32, name="bs23", tag="in2", align_bytes=64)
+        for j in range(2):
+            nc.sync.dma_start(out=bs01[j][:], in_=base[:, cols(j)])
+        nc.sync.dma_start(out=bs23[:], in_=base[:, 2 * BANK :])
+        bs = [bs01[0][:], bs01[1][:], bs23[:, 0:BANK], bs23[:, BANK:]]
+
+        a_sb = sb.tile([P, V], F32, name="a_sb")
+        t_sb = sb.tile([P, V], F32, name="t_sb")
+        mx = sb.tile([P, NB], F32, name="mx")
+        for j in range(NB):
+            nc.vector.tensor_scalar(out=a_sb[:, cols(j)], in0=pa[j][:], scalar1=1.0, scalar2=None, op0=mult,
+                                    op1=ALU.max, accum_out=mx[:, j : j + 1])
+        negm = sb.tile([P, 1], F32, name="negm")
+        nc.vector.tensor_reduce(out=negm[:], in_=mx[:], axis=AX.X, op=ALU.max, negate=True)
+        ag1 = sb.tile([P, NL], F32, name="ag1")
+        ag2 = sb.tile([P, NL], F32, name="ag2")
+        nc.vector.tensor_copy(out=ag1[:], in_=a_sb[:].indirect(o1[:]))
+        nc.vector.tensor_copy(out=ag2[:], in_=a_sb[:].indirect(o2[:]))
+        nc.vector.tensor_scalar(out=inp[:, 0:1], in0=stk[:], scalar1=8192.0, scalar2=None, op0=mult)
+
+        p = sb.tile([P, V], F32, name="p")
+        z = sb.tile([P, 1], F32, name="z")
+        s1 = sb.tile([P, 1], F32, name="s1")
+        s2 = sb.tile([P, 1], F32, name="s2")
+        px1 = sb.tile([P, NL], F32, name="px1")
+        px2 = sb.tile([P, NL], F32, name="px2")
+        nc.scalar.copy(out=t_sb[:, cols(0)], in_=pt[0][:])
+        nc.scalar.activation(out=p[:], in_=a_sb[:], func=ACT.Exp, bias=negm[:], accum_out=z[:])
+
+        xx = sb.tile([P, 5], F32, name="xx")
+        cc = sb.tile([P, 4], F32, name="cc")
+        xp = sb.tile([P, V], F32, name="xp")
+        xzp = sb.tile([P, NB], F32, name="xzp")
+        r = xx[:, 3:4]
+
+        def scaled(dst, src, scale):
+            nc.scalar.activation(out=dst, in_=src, func=ACT.Copy, scale=scale)
+
+        def affine(dst, src, scale, bias):
+            nc.scalar.activation(out=dst, in_=src, func=ACT.Identity, scale=scale, bias=bias)
+
+        def dense_product(j):
+            nc.vector.scalar_tensor_tensor(out=xp[:, cols(j)], in0=pt[j][:], scalar=-0.125, in1=p[:, cols(j)],
+                                           op0=mult, op1=mult, accum_out=xzp[:, j : j + 1])
+
+        den = sb.tile([P, 1], F32, name="den")
+        g = sb.tile([P, 1], F32, name="g")
+        bb = sb.tile([P, 5], F32, name="bb")
+        gn = sb.tile([P, 1], F32, name="gn")
+        fr = sb.tile([P, 1], F32, name="fr")
+        be = sb.tile([P, 1], F32, name="be")
+        nc.scalar.activation(out=px1[:], in_=ag1[:], func=ACT.Exp, bias=negm[:], accum_out=s1[:])
+        nc.scalar.activation(out=px2[:], in_=ag2[:], func=ACT.Exp, bias=negm[:], accum_out=s2[:])
+        nc.vector.reciprocal(out=r, in_=z[:])
+        dense_product(0)
+        nc.vector.tensor_scalar(out=cc[:], in0=inp[:], scalar1=r, scalar2=None, op0=mult)
+        nc.vector.tensor_scalar(out=xx[:, 0:3], in0=inp[:, 0:3], scalar1=r, scalar2=r, op0=mult, op1=mult)
+        scaled(xx[:, 4:5], xx[:, 1:2], s1[:])
+        scaled(yy[:, 0:2], xx[:, 2:4], s1[:])
+        nc.scalar.copy(out=t_sb[:, cols(3)], in_=pt[3][:])
+        affine(den[:], s2[:], xx[:, 4:5], one[:])
+        scaled(yy[:, 3:6], xx[:, 2:5], s2[:])
+        dense_product(1)
+        nc.scalar.copy(out=t_sb[:, cols(1)], in_=pt[1][:])
+        dense_product(2)
+        nc.scalar.copy(out=t_sb[:, cols(2)], in_=pt[2][:])
+        nc.vector.reciprocal(out=g[:], in_=den[:])
+        dense_product(3)
+        nc.vector.tensor_scalar(out=bb[:], in0=yy[:, 1:6], scalar1=cc[:, 0:1], scalar2=g[:], op0=mult, op1=mult)
+        tz = sb.tile([P, 1], F32, name="tz")
+        nc.vector.tensor_reduce(out=tz[:], in_=xzp[:], axis=AX.X, op=add)
+
+        xpx1 = sb.tile([P, NL], F32, name="xpx1")
+        xpx2 = sb.tile([P, NL], F32, name="xpx2")
+        nc.vector.tensor_tensor(out=xpx1[:], in0=t_sb[:].indirect(o1[:]), in1=px1[:], op=mult)
+        nc.vector.tensor_scalar(out=yy[:, 7:10], in0=cc[:, 1:4], scalar1=tz[:], scalar2=None, op0=mult)
+        nc.vector.tensor_scalar(out=gn[:], in0=yy[:, 0:1], scalar1=g[:], scalar2=None, op0=mult)
+        nc.vector.tensor_scalar(out=fr[:], in0=xx[:, 0:1], scalar1=g[:], scalar2=None, op0=mult)
+        nc.vector.tensor_tensor(out=xpx2[:], in0=t_sb[:].indirect(o2[:]), in1=px2[:], op=mult)
+
+        w1 = sb.tile([P, NL], F32, name="w1")
+        w2 = sb.tile([P, NL], F32, name="w2")
+        t1 = sb.tile([P, 1], F32, name="t1")
+        t2 = sb.tile([P, 1], F32, name="t2")
+        uu = sb.tile([P, 2], F32, name="uu")
+        a1 = [sb.tile([P, BANK], F32, name=f"a1_{j}") for j in range(NB)]
+        a2 = [sb.tile([P, BANK], F32, name=f"a2_{j}") for j in range(NB)]
+        for j in range(2):
+            scaled(a2[j][:], xp[:, cols(j)], bb[:, 4:5])
+        nc.scalar.activation(out=xp[:, cols(1)], in_=xpx1[:], func=ACT.Copy, accum_out=t1[:])
+        scaled(w1[:], xpx1[:], bb[:, 3:4])
+        nc.scalar.activation(out=xpx1[:], in_=xpx2[:], func=ACT.Copy, accum_out=t2[:])
+        nc.vector.tensor_scalar(out=yy[:, 6:7], in0=yy[:, 5:6], scalar1=yy[:, 8:9], scalar2=None, op0=mult)
+        nc.vector.tensor_scalar(out=be[:], in0=gn[:], scalar1=bb[:, 3:4], scalar2=fr[:], op0=mult, op1=add)
+        nc.vector.scalar_tensor_tensor(out=uu[:], in0=yy[:, 3:4].to_broadcast([P, 2]), scalar=t1[:], in1=yy[:, 6:8],
+                                       op0=mult, op1=add)
+
+        gu = sb.tile([P, 2], F32, name="gu")
+        ft = sb.tile([P, 1], F32, name="ft")
+        zb = sb.tile([P, 1], F32, name="zb")
+        al = sb.tile([P, 1], F32, name="al")
+        c1 = sb.tile([P, 1], F32, name="c1")
+        nc.vector.tensor_scalar(out=zb[:], in0=yy[:, 9:10], scalar1=bb[:, 4:5], scalar2=None, op0=mult)
+        nc.vector.tensor_scalar(out=ft[:], in0=t1[:], scalar1=fr[:], scalar2=None, op0=mult)
+        nc.vector.tensor_scalar(out=gu[:], in0=uu[:], scalar1=g[:], scalar2=None, op0=mult)
+        nc.vector.tensor_scalar(out=al[:], in0=uu[:, 1:2], scalar1=bb[:, 3:4], scalar2=g[:], op0=mult, op1=mult)
+        nc.vector.tensor_scalar(out=c1[:], in0=t2[:], scalar1=be[:], scalar2=al[:], op0=mult, op1=add)
+        v1 = sb.tile([P, NL], F32, name="v1")
+        v2 = sb.tile([P, NL], F32, name="v2")
+        nc.vector.tensor_scalar(out=v1[:], in0=px1[:], scalar1=c1[:], scalar2=None, op0=mult)
+        nc.vector.tensor_tensor(out=xs2[:].indirect(o1[:]), in0=v1[:], in1=w1[:], op=add)
+
+        qq = sb.tile([P, 1], F32, name="qq")
+        negh = sb.tile([P, 1], F32, name="negh")
+        c0 = sb.tile([P, 1], F32, name="c0")
+        c2 = sb.tile([P, 1], F32, name="c2")
+        affine(qq[:], t2[:], gn[:], gu[:, 0:1])
+        affine(negh[:], t2[:], gn[:], gu[:, 1:2])
+        scaled(a2[2][:], xp[:, cols(2)], bb[:, 4:5])
+        affine(c0[:], qq[:], bb[:, 1:2], zb[:])
+        affine(c2[:], negh[:], bb[:, 0:1], ft[:])
+        scaled(a2[3][:], xp[:, cols(3)], bb[:, 4:5])
+        for j in range(2):
+            scaled(a1[j][:], p[:, cols(j)], c0[:])
+        scaled(w2[:], xpx2[:], bb[:, 0:1])
+        scaled(v2[:], px2[:], c2[:])
+        for j in range(2, NB):
+            scaled(a1[j][:], p[:, cols(j)], c0[:])
+        nc.vector.tensor_tensor(out=xs1[:].indirect(o2[:]), in0=v2[:], in1=w2[:], op=add)
+
+        st1 = [ps.tile([P, BANK], F32, name=f"st{j}", tag=f"pa{j}") for j in range(NB)]
+
+        def turn_add(j, src, first, last):
+            for k in range(4):
+                blk = slice(k * P, (k + 1) * P)
+                nc.tensor.matmul(st1[j][:, blk], lhsT=src[:, blk], rhs=ident[:], is_transpose=True,
+                                 start=(first and k == 0), stop=(last and k == 3))
+
+        for j in range(NB):
+            turn_add(j, bs[j], True, False)
+        for j in range(NB):
+            turn_add(j, a2[j][:], False, False)
+        for j in range(NB):
+            turn_add(j, a1[j][:], False, False)
+        back = []
+        for j in range(NB):
+            turn_add(j, xs2[:, cols(j)], False, True)
+            dt = sb.tile([P, BANK], F32, name=f"dt{j}")
+            nc.scalar.copy(out=dt[:], in_=st1[j][:])
+            bk = ps.tile([P, BANK], F32, name=f"bk{j}", tag=f"pt{j}")
+            for k in range(4):
+                blk = slice(k * P, (k + 1) * P)
+                nc.tensor.transpose(bk[:, blk], dt[:, blk], ident[:])
+            back.append(bk)
+        pieces = [(j, 0, BANK) for j in range(NB - 1)] + [(NB - 1, 0, BANK // 2), (NB - 1, BANK // 2, BANK)]
+        for n, (j, lo, hi) in enumerate(pieces):
+            res = sb.tile([P, hi - lo], F32, name=f"res{n}")
+            span = slice(j * BANK + lo, j * BANK + hi)
+            nc.vector.tensor_tensor(out=res[:], in0=back[j][:, lo:hi], in1=xs1[:, span], op=add)
+            nc.sync.dma_start(out=out[:, span], in_=res[:])

@@ -21,6 +21,7 @@ AX = mybir.AxisListType
 P = 128
 BANK = 512
 NB = V // BANK
+VEC_BANKS = 1
 
 
 def tile_attend_hvjointcover_heads_kernel(tc, hid, voc_words, voc_scales, stake, dhid, base, offs, offs2, out):
@@ -55,12 +56,6 @@ def tile_attend_hvjointcover_heads_kernel(tc, hid, voc_words, voc_scales, stake,
         nc.sync.dma_start(o1[:], offs)
         nc.sync.dma_start(o2[:], offs2)
 
-        inp = sb.tile([P, 4], F32, name="inp")
-        nc.vector.memset(inp[:, 1:2], 16.0)
-        nc.vector.memset(inp[:, 2:3], -16.0)
-        nc.vector.memset(inp[:, 3:4], -1.0)
-        yy = sb.tile([P, 10], F32, name="yy")
-        nc.vector.memset(yy[:, 2:3], 0.125)
         xs2 = sb.tile([P, V], F32, name="xs2")
         nc.vector.memset(xs2[:], 0.0)
         ident = sb.tile([P, P], F32, name="ident")
@@ -77,6 +72,8 @@ def tile_attend_hvjointcover_heads_kernel(tc, hid, voc_words, voc_scales, stake,
         nc.scalar.copy(out=dg[:], in_=draw[:].rearrange("p j q -> p q j"))
         nc.vector.quantize_mx(out=dq[:].bitcast(FP8X4), scales=ds[:], in_=dg[:].rearrange("p q j -> p (q j)"))
 
+        inp = sb.tile([P, 3], F32, name="inp")
+        nc.vector.memset(inp[:, 0:1], -16.0)
         xs1 = sb.tile([P, V], F32, name="xs1", tag="dg", align_bytes=64)
         nc.gpsimd.memset(xs1[:], 0.0)
 
@@ -102,155 +99,152 @@ def tile_attend_hvjointcover_heads_kernel(tc, hid, voc_words, voc_scales, stake,
         nc.sync.dma_start(out=bs23[:], in_=base[:, 2 * BANK :])
         bs = [bs01[0][:], bs01[1][:], bs23[:, 0:BANK], bs23[:, BANK:]]
 
-        a_sb = sb.tile([P, V], F32, name="a_sb")
-        t_sb = sb.tile([P, V], F32, name="t_sb")
-        mx = sb.tile([P, NB], F32, name="mx")
-        for j in range(NB):
-            nc.vector.tensor_scalar(out=a_sb[:, cols(j)], in0=pa[j][:], scalar1=1.0, scalar2=None, op0=mult,
-                                    op1=ALU.max, accum_out=mx[:, j : j + 1])
-        negm = sb.tile([P, 1], F32, name="negm")
-        nc.vector.tensor_reduce(out=negm[:], in_=mx[:], axis=AX.X, op=ALU.max, negate=True)
-        ag1 = sb.tile([P, NL], F32, name="ag1")
-        ag2 = sb.tile([P, NL], F32, name="ag2")
-        nc.vector.tensor_copy(out=ag1[:], in_=a_sb[:].indirect(o1[:]))
-        nc.vector.tensor_copy(out=ag2[:], in_=a_sb[:].indirect(o2[:]))
-        nc.vector.tensor_scalar(out=inp[:, 0:1], in0=stk[:], scalar1=8192.0, scalar2=None, op0=mult)
-
-        p = sb.tile([P, V], F32, name="p")
-        z = sb.tile([P, 1], F32, name="z")
-        s1 = sb.tile([P, 1], F32, name="s1")
-        s2 = sb.tile([P, 1], F32, name="s2")
-        px1 = sb.tile([P, NL], F32, name="px1")
-        px2 = sb.tile([P, NL], F32, name="px2")
-        nc.scalar.copy(out=t_sb[:, cols(0)], in_=pt[0][:])
-        nc.scalar.activation(out=p[:], in_=a_sb[:], func=ACT.Exp, bias=negm[:], accum_out=z[:])
-
-        xx = sb.tile([P, 5], F32, name="xx")
-        cc = sb.tile([P, 4], F32, name="cc")
-        xp = sb.tile([P, V], F32, name="xp")
-        xzp = sb.tile([P, NB], F32, name="xzp")
-        r = xx[:, 3:4]
-
         def scaled(dst, src, scale):
             nc.scalar.activation(out=dst, in_=src, func=ACT.Copy, scale=scale)
 
         def affine(dst, src, scale, bias):
             nc.scalar.activation(out=dst, in_=src, func=ACT.Identity, scale=scale, bias=bias)
 
-        def dense_product(j):
-            nc.vector.scalar_tensor_tensor(out=xp[:, cols(j)], in0=pt[j][:], scalar=-0.125, in1=p[:, cols(j)],
-                                           op0=mult, op1=mult, accum_out=xzp[:, j : j + 1])
+        def ts(dst, src, s1_, s2_=None, op1=None):
+            if s2_ is None:
+                nc.vector.tensor_scalar(out=dst, in0=src, scalar1=s1_, scalar2=None, op0=mult)
+            else:
+                nc.vector.tensor_scalar(out=dst, in0=src, scalar1=s1_, scalar2=s2_, op0=mult, op1=op1)
 
-        den = sb.tile([P, 1], F32, name="den")
-        g = sb.tile([P, 1], F32, name="g")
-        bb = sb.tile([P, 5], F32, name="bb")
-        gn = sb.tile([P, 1], F32, name="gn")
-        fr = sb.tile([P, 1], F32, name="fr")
-        be = sb.tile([P, 1], F32, name="be")
-        nc.scalar.activation(out=px1[:], in_=ag1[:], func=ACT.Exp, bias=negm[:], accum_out=s1[:])
-        nc.scalar.activation(out=px2[:], in_=ag2[:], func=ACT.Exp, bias=negm[:], accum_out=s2[:])
-        nc.vector.reciprocal(out=r, in_=z[:])
-        dense_product(0)
-        nc.vector.tensor_scalar(out=cc[:], in0=inp[:], scalar1=r, scalar2=None, op0=mult)
-        nc.vector.tensor_scalar(out=xx[:, 0:3], in0=inp[:, 0:3], scalar1=r, scalar2=r, op0=mult, op1=mult)
-        scaled(xx[:, 4:5], xx[:, 1:2], s1[:])
-        scaled(yy[:, 0:2], xx[:, 2:4], s1[:])
-        nc.scalar.copy(out=t_sb[:, cols(3)], in_=pt[3][:])
-        affine(den[:], s2[:], xx[:, 4:5], one[:])
-        scaled(yy[:, 3:6], xx[:, 2:5], s2[:])
-        dense_product(1)
-        nc.scalar.copy(out=t_sb[:, cols(1)], in_=pt[1][:])
-        dense_product(2)
-        nc.scalar.copy(out=t_sb[:, cols(2)], in_=pt[2][:])
-        nc.vector.reciprocal(out=g[:], in_=den[:])
-        dense_product(3)
-        nc.vector.tensor_scalar(out=bb[:], in0=yy[:, 1:6], scalar1=cc[:, 0:1], scalar2=g[:], op0=mult, op1=mult)
-        tz = sb.tile([P, 1], F32, name="tz")
-        nc.vector.tensor_reduce(out=tz[:], in_=xzp[:], axis=AX.X, op=add)
+        def col(name, width=1):
+            return sb.tile([P, width], F32, name=name)
 
+        a_sb = sb.tile([P, V], F32, name="a_sb")
+        t_sb = sb.tile([P, V], F32, name="t_sb")
+        p = sb.tile([P, V], F32, name="p", tag="p")
+        mx, zp = col("mx", NB), col("zp", 3)
+        for j in range(NB):
+            nc.vector.tensor_scalar(out=a_sb[:, cols(j)], in0=pa[j][:], scalar1=1.0, scalar2=None, op0=mult,
+                                    op1=ALU.max, accum_out=mx[:, j : j + 1])
+        negm = col("negm")
+        nc.vector.tensor_reduce(out=negm[:], in_=mx[:], axis=AX.X, op=ALU.max, negate=True)
+        for j in range(NB - 1):
+            nc.scalar.copy(out=t_sb[:, cols(j)], in_=pt[j][:])
+        nc.vector.tensor_scalar(out=inp[:, 1:2], in0=stk[:], scalar1=8192.0, scalar2=one[:], op0=mult, op1=mult)
+        ts(inp[:, 2:3], stk[:], -16384.0)
+        ag1 = sb.tile([P, NL], F32, name="ag1")
+        ag2 = sb.tile([P, NL], F32, name="ag2")
+        px1 = sb.tile([P, NL], F32, name="px1")
+        px2 = sb.tile([P, NL], F32, name="px2")
+        nc.vector.tensor_copy(out=ag1[:], in_=a_sb[:].indirect(o1[:]))
+        nc.vector.tensor_copy(out=ag2[:], in_=a_sb[:].indirect(o2[:]))
+        nc.vector.tensor_copy(out=t_sb[:, cols(NB - 1)], in_=pt[NB - 1][:])
+
+        ss, den, rec = col("ss", 2), col("den", 4), col("rec", 4)
+        s1, s2, z = ss[:, 0:1], ss[:, 1:2], den[:, 1:2]
+        yy = col("yy", 8)
+        qq, gg, bdn = col("qq"), col("gg", 7), col("bdn")
+
+        def dense_exp(lo, hi, n):
+            nc.scalar.activation(out=p[:, lo:hi], in_=a_sb[:, lo:hi], func=ACT.Exp, bias=negm[:], accum_out=zp[:, n : n + 1])
+
+        sg = sb.tile([P, 1], F32, name="sg", tag="w")
+        za = col("za")
+        dense_exp(0, 2 * BANK, 0)
+        nc.scalar.activation(out=px1[:], in_=ag1[:], func=ACT.Exp, bias=negm[:], accum_out=s1)
+        dense_exp(2 * BANK, 3 * BANK, 1)
+        nc.scalar.activation(out=px2[:], in_=ag2[:], func=ACT.Exp, bias=negm[:], accum_out=s2)
+        scaled(yy[:, 5:8], inp[:], s1)
+        affine(za[:], zp[:, 0:1], 1.0, zp[:, 1:2])
+        dense_exp(3 * BANK, V, 2)
+        ts(sg[:], s1, s2, 16.0, mult)
+        scaled(yy[:, 0:2], inp[:, 0:2], s2)
+        scaled(qq[:], yy[:, 7:8], s2)
+        nc.scalar.activation(out=den[:, 2:4], in_=ss[:], func=ACT.Copy, bias=1e-30)
+        affine(z, zp[:, 2:3], 1.0, za[:])
+        affine(den[:, 0:1], z, z, sg[:])
         xpx1 = sb.tile([P, NL], F32, name="xpx1")
         xpx2 = sb.tile([P, NL], F32, name="xpx2")
         nc.vector.tensor_tensor(out=xpx1[:], in0=t_sb[:].indirect(o1[:]), in1=px1[:], op=mult)
-        nc.vector.tensor_scalar(out=yy[:, 7:10], in0=cc[:, 1:4], scalar1=tz[:], scalar2=None, op0=mult)
-        nc.vector.tensor_scalar(out=gn[:], in0=yy[:, 0:1], scalar1=g[:], scalar2=None, op0=mult)
-        nc.vector.tensor_scalar(out=fr[:], in0=xx[:, 0:1], scalar1=g[:], scalar2=None, op0=mult)
         nc.vector.tensor_tensor(out=xpx2[:], in0=t_sb[:].indirect(o2[:]), in1=px2[:], op=mult)
+        ts(yy[:, 2:3], inp[:, 1:2], 1.0)
+        nc.vector.reciprocal(out=rec[:], in_=den[:])
+        idd, r = rec[:, 0:1], rec[:, 1:2]
+        ts(bdn[:], qq[:], idd, r, mult)
+        scaled(yy[:, 3:4], z, z)
+        scaled(yy[:, 4:5], z, -2.0)
 
-        w1 = sb.tile([P, NL], F32, name="w1")
-        w2 = sb.tile([P, NL], F32, name="w2")
-        t1 = sb.tile([P, 1], F32, name="t1")
-        t2 = sb.tile([P, 1], F32, name="t2")
-        uu = sb.tile([P, 2], F32, name="uu")
-        a1 = [sb.tile([P, BANK], F32, name=f"a1_{j}") for j in range(NB)]
-        a2 = [sb.tile([P, BANK], F32, name=f"a2_{j}") for j in range(NB)]
-        for j in range(2):
-            scaled(a2[j][:], xp[:, cols(j)], bb[:, 4:5])
-        nc.scalar.activation(out=xp[:, cols(1)], in_=xpx1[:], func=ACT.Copy, accum_out=t1[:])
-        scaled(w1[:], xpx1[:], bb[:, 3:4])
-        nc.scalar.activation(out=xpx1[:], in_=xpx2[:], func=ACT.Copy, accum_out=t2[:])
-        nc.vector.tensor_scalar(out=yy[:, 6:7], in0=yy[:, 5:6], scalar1=yy[:, 8:9], scalar2=None, op0=mult)
-        nc.vector.tensor_scalar(out=be[:], in0=gn[:], scalar1=bb[:, 3:4], scalar2=fr[:], op0=mult, op1=add)
-        nc.vector.scalar_tensor_tensor(out=uu[:], in0=yy[:, 3:4].to_broadcast([P, 2]), scalar=t1[:], in1=yy[:, 6:8],
-                                       op0=mult, op1=add)
+        a2 = sb.tile([P, V], F32, name="a2")
+        xzp = col("xzp", NB)
+        for j in range(NB):
+            nc.vector.scalar_tensor_tensor(out=a2[:, cols(j)], in0=pt[j][:], scalar=bdn[:], in1=p[:, cols(j)],
+                                           op0=mult, op1=mult, accum_out=xzp[:, j : j + 1])
 
-        gu = sb.tile([P, 2], F32, name="gu")
-        ft = sb.tile([P, 1], F32, name="ft")
-        zb = sb.tile([P, 1], F32, name="zb")
-        al = sb.tile([P, 1], F32, name="al")
-        c1 = sb.tile([P, 1], F32, name="c1")
-        nc.vector.tensor_scalar(out=zb[:], in0=yy[:, 9:10], scalar1=bb[:, 4:5], scalar2=None, op0=mult)
-        nc.vector.tensor_scalar(out=ft[:], in0=t1[:], scalar1=fr[:], scalar2=None, op0=mult)
-        nc.vector.tensor_scalar(out=gu[:], in0=uu[:], scalar1=g[:], scalar2=None, op0=mult)
-        nc.vector.tensor_scalar(out=al[:], in0=uu[:, 1:2], scalar1=bb[:, 3:4], scalar2=g[:], op0=mult, op1=mult)
-        nc.vector.tensor_scalar(out=c1[:], in0=t2[:], scalar1=be[:], scalar2=al[:], op0=mult, op1=add)
+        ww = sb.tile([P, 2 * NL], F32, name="ww", tag="w")
+        w1, w2 = ww[:, :NL], ww[:, NL:]
+        tt = col("tt", 2)
+        t1, t2 = tt[:, 0:1], tt[:, 1:2]
+        nc.scalar.activation(out=w1, in_=xpx1[:], func=ACT.Copy, accum_out=t1)
+        scaled(gg[:], yy[:, 0:7], idd)
+        gs2, b1, aa, g, nz2, gs1, b2 = (gg[:, n : n + 1] for n in range(7))
+        nc.scalar.activation(out=w2, in_=xpx2[:], func=ACT.Copy, accum_out=t2)
+        ag, e1, e2, be12, be0, h1 = col("ag"), col("e1"), col("e2"), col("be12", 2), col("be0"), col("h1")
+        agt, h2, al1, al2, al0 = col("agt", 2), col("h2"), col("al1"), col("al2"), col("al0")
+        scaled(ag[:], aa, g)
+        scaled(e1[:], b1, gs2)
+        scaled(e2[:], b2, gs1)
+        scaled(be12[:], rec[:, 2:4], g)
+        affine(be0[:], r, -1.0, nz2)
+        scaled(h1[:], t1, b1)
+        scaled(agt[:], tt[:], ag[:])
+        affine(h2[:], t2, b2, h1[:])
+        scaled(w1, xpx1[:], b1)
+        affine(al1[:], t1, e1[:], agt[:, 1:2])
+        affine(al2[:], t2, e2[:], agt[:, 0:1])
+        scaled(al0[:], h2[:], nz2)
+        scaled(w2, xpx2[:], b2)
+
+        c1, c0, c2, cj = col("c1"), col("c0"), col("c2"), col("cj", 3 * NB)
+        for n, (c, be, al) in enumerate(((c1, be12[:, 0:1], al1), (c0, be0[:], al0), (c2, be12[:, 1:2], al2))):
+            nc.vector.tensor_scalar(out=cj[:, n * NB : (n + 1) * NB], in0=xzp[:], scalar1=be, scalar2=al[:], op0=mult, op1=add,
+                                    accum_out=c[:])
         v1 = sb.tile([P, NL], F32, name="v1")
         v2 = sb.tile([P, NL], F32, name="v2")
-        nc.vector.tensor_scalar(out=v1[:], in0=px1[:], scalar1=c1[:], scalar2=None, op0=mult)
-        nc.vector.tensor_tensor(out=xs2[:].indirect(o1[:]), in0=v1[:], in1=w1[:], op=add)
-
-        qq = sb.tile([P, 1], F32, name="qq")
-        negh = sb.tile([P, 1], F32, name="negh")
-        c0 = sb.tile([P, 1], F32, name="c0")
-        c2 = sb.tile([P, 1], F32, name="c2")
-        affine(qq[:], t2[:], gn[:], gu[:, 0:1])
-        affine(negh[:], t2[:], gn[:], gu[:, 1:2])
-        scaled(a2[2][:], xp[:, cols(2)], bb[:, 4:5])
-        affine(c0[:], qq[:], bb[:, 1:2], zb[:])
-        affine(c2[:], negh[:], bb[:, 0:1], ft[:])
-        scaled(a2[3][:], xp[:, cols(3)], bb[:, 4:5])
-        for j in range(2):
+        ts(v1[:], px1[:], c1[:])
+        nc.vector.tensor_tensor(out=xs2[:].indirect(o1[:]), in0=v1[:], in1=w1, op=add)
+        a1 = [sb.tile([P, BANK], F32, name=f"a1_{j}") for j in range(NB)]
+        for j in range(NB):
             scaled(a1[j][:], p[:, cols(j)], c0[:])
-        scaled(w2[:], xpx2[:], bb[:, 0:1])
         scaled(v2[:], px2[:], c2[:])
-        for j in range(2, NB):
-            scaled(a1[j][:], p[:, cols(j)], c0[:])
-        nc.vector.tensor_tensor(out=xs1[:].indirect(o2[:]), in0=v2[:], in1=w2[:], op=add)
+        nc.vector.tensor_tensor(out=xs1[:].indirect(o2[:]), in0=v2[:], in1=w2, op=add)
 
         st1 = [ps.tile([P, BANK], F32, name=f"st{j}", tag=f"pa{j}") for j in range(NB)]
 
-        def turn_add(j, src, first, last):
+        def turn_add(j, src, first, last, eye=ident):
             for k in range(4):
                 blk = slice(k * P, (k + 1) * P)
-                nc.tensor.matmul(st1[j][:, blk], lhsT=src[:, blk], rhs=ident[:], is_transpose=True,
+                nc.tensor.matmul(st1[j][:, blk], lhsT=src[:, blk], rhs=eye[:], is_transpose=True,
                                  start=(first and k == 0), stop=(last and k == 3))
 
         for j in range(NB):
             turn_add(j, bs[j], True, False)
         for j in range(NB):
-            turn_add(j, a2[j][:], False, False)
+            turn_add(j, a2[:, cols(j)], False, False)
         for j in range(NB):
-            turn_add(j, a1[j][:], False, False)
+            turn_add(j, a1[j][:], False, j < VEC_BANKS)
+        ident2 = sb.tile([P, P], F32, name="ident2", tag="p")
+        nc.scalar.copy(out=ident2[:], in_=ident[:])
         back = []
         for j in range(NB):
-            turn_add(j, xs2[:, cols(j)], False, True)
+            if j >= VEC_BANKS:
+                turn_add(j, xs2[:, cols(j)], False, True, ident2)
             dt = sb.tile([P, BANK], F32, name=f"dt{j}")
             nc.scalar.copy(out=dt[:], in_=st1[j][:])
             bk = ps.tile([P, BANK], F32, name=f"bk{j}", tag=f"pt{j}")
             for k in range(4):
                 blk = slice(k * P, (k + 1) * P)
                 nc.tensor.transpose(bk[:, blk], dt[:, blk], ident[:])
-            back.append(bk)
-        pieces = [(j, 0, BANK) for j in range(NB - 1)] + [(NB - 1, 0, BANK // 2), (NB - 1, BANK // 2, BANK)]
+            back.append(bk[:])
+        for j in range(VEC_BANKS):
+            part = sb.tile([P, BANK], F32, name=f"part{j}")
+            nc.vector.tensor_tensor(out=part[:], in0=back[j], in1=xs2[:, cols(j)], op=add)
+            back[j] = part[:]
+        pieces = [(j, 0, BANK) for j in (1, 0, 2)] + [(NB - 1, 0, BANK // 2), (NB - 1, BANK // 2, BANK)]
         for n, (j, lo, hi) in enumerate(pieces):
             res = sb.tile([P, hi - lo], F32, name=f"res{n}")
             span = slice(j * BANK + lo, j * BANK + hi)

@@ -43,14 +43,16 @@ def tile_attend_hvjointcover_heads_kernel(tc, hid, voc_words, voc_scales, stake,
         nc.scalar.activation(out=one[:], in_=zero[:], func=ACT.Exp)
 
         hraw = sb.tile([P, 4, Q], F32, name="hraw", tag="in0", align_bytes=64)
-        words = sb.tile([P, 2 * V], U8, name="words", tag="in2", align_bytes=64)
+        words = [sb.tile([P, V], U8, name=f"words{h}", tag=f"in{2 + h}", align_bytes=64) for h in range(2)]
+        w32 = voc_words[0].bitcast(I32)
         nc.sync.dma_start(out=hraw[:], in_=hid.rearrange("(p j) q -> p j q", j=4))
-        nc.sync.dma_start(out=words[:].bitcast(I32), in_=voc_words[0].bitcast(I32))
         s32 = voc_scales[0].bitcast(I32)
         for g in range(4):
             nc.sync.dma_start(out=vsc[32 * g : 32 * g + 4, :].bitcast(I32), in_=s32[4 * g : 4 * g + 4, :])
+        nc.sync.dma_start(out=words[0][:].bitcast(I32), in_=w32[:, :BANK])
         draw = sb.tile([P, 4, Q], F32, name="draw", tag="in1", align_bytes=64)
         nc.sync.dma_start(out=draw[:], in_=dhid.rearrange("(p j) q -> p j q", j=4))
+        nc.sync.dma_start(out=words[1][:].bitcast(I32), in_=w32[:, BANK:])
         o1 = lists.tile([P, NL // 16], U16, name="o1")
         o2 = lists.tile([P, NL // 16], U16, name="o2")
         nc.sync.dma_start(o1[:], offs)
@@ -74,30 +76,27 @@ def tile_attend_hvjointcover_heads_kernel(tc, hid, voc_words, voc_scales, stake,
 
         inp = sb.tile([P, 3], F32, name="inp")
         nc.vector.memset(inp[:, 0:1], -16.0)
-        xs1 = sb.tile([P, V], F32, name="xs1", tag="dg", align_bytes=64)
-        nc.gpsimd.memset(xs1[:], 0.0)
 
-        def scores(codes, scales, tag):
+        def scores(codes, scales, name, where):
             banks = []
             for j in range(NB):
-                b = ps.tile([P, BANK], F32, name=f"{tag}{j}", tag=f"{tag}{j}")
-                wj = words[:, 2 * j * BANK : 2 * (j + 1) * BANK]
+                b = ps.tile([P, BANK], F32, name=f"{name}{j}", tag=f"bank{where[j]}")
+                wj = words[j // 2][:, (j % 2) * 2 * BANK : (j % 2 + 1) * 2 * BANK]
                 nc.tensor.matmul_mx(out=b[:], lhsT=codes[:].bitcast(FP8X4), lhsT_scale=scales[:],
                                     rhs=wj.bitcast(FP4X4), rhs_scale=vsc[:, cols(j)], start=True, stop=True)
                 banks.append(b)
             return banks
 
-        pa = scores(hq, hs, "pa")
-        pt = scores(dq, ds, "pt")
+        pa = scores(hq, hs, "pa", (0, 1, 2, 3))
+        xs1 = sb.tile([P, V], F32, name="xs1", tag="hg", align_bytes=64)
+        nc.gpsimd.memset(xs1[:], 0.0)
+        pt = scores(dq, ds, "pt", (4, 5, 6, 3))
 
-        stk = sb.tile([P, 1], F32, name="stk", tag="hg", align_bytes=64)
+        stk = sb.tile([P, 1], F32, name="stk", tag="dg", align_bytes=64)
         nc.sync.dma_start(out=stk[:], in_=stake)
-        bs01 = [sb.tile([P, BANK], F32, name=f"bs{j}", tag=f"in{j}", align_bytes=64) for j in range(2)]
-        bs23 = sb.tile([P, 2 * BANK], F32, name="bs23", tag="in2", align_bytes=64)
-        for j in range(2):
-            nc.sync.dma_start(out=bs01[j][:], in_=base[:, cols(j)])
-        nc.sync.dma_start(out=bs23[:], in_=base[:, 2 * BANK :])
-        bs = [bs01[0][:], bs01[1][:], bs23[:, 0:BANK], bs23[:, BANK:]]
+        bs = [sb.tile([P, BANK], F32, name=f"bs{j}", tag=f"in{j}", align_bytes=64) for j in range(NB)]
+        for j in range(NB):
+            nc.sync.dma_start(out=bs[j][:], in_=base[:, cols(j)])
 
         def scaled(dst, src, scale):
             nc.scalar.activation(out=dst, in_=src, func=ACT.Copy, scale=scale)
@@ -207,13 +206,7 @@ def tile_attend_hvjointcover_heads_kernel(tc, hid, voc_words, voc_scales, stake,
         v2 = sb.tile([P, NL], F32, name="v2")
         ts(v1[:], px1[:], c1[:])
         nc.vector.tensor_tensor(out=xs2[:].indirect(o1[:]), in0=v1[:], in1=w1, op=add)
-        a1 = [sb.tile([P, BANK], F32, name=f"a1_{j}") for j in range(NB)]
-        for j in range(NB):
-            scaled(a1[j][:], p[:, cols(j)], c0[:])
-        scaled(v2[:], px2[:], c2[:])
-        nc.vector.tensor_tensor(out=xs1[:].indirect(o2[:]), in0=v2[:], in1=w2, op=add)
-
-        st1 = [ps.tile([P, BANK], F32, name=f"st{j}", tag=f"pa{j}") for j in range(NB)]
+        st1 = [ps.tile([P, BANK], F32, name=f"st{j}", tag=f"bank{(0, 1, 2, 7)[j]}") for j in range(NB)]
 
         def turn_add(j, src, first, last, eye=ident):
             for k in range(4):
@@ -222,28 +215,36 @@ def tile_attend_hvjointcover_heads_kernel(tc, hid, voc_words, voc_scales, stake,
                                  start=(first and k == 0), stop=(last and k == 3))
 
         for j in range(NB):
-            turn_add(j, bs[j], True, False)
+            turn_add(j, bs[j][:], True, False)
         for j in range(NB):
             turn_add(j, a2[:, cols(j)], False, False)
-        for j in range(NB):
-            turn_add(j, a1[j][:], False, j < VEC_BANKS)
-        ident2 = sb.tile([P, P], F32, name="ident2", tag="p")
-        nc.scalar.copy(out=ident2[:], in_=ident[:])
-        back = []
-        for j in range(NB):
-            if j >= VEC_BANKS:
-                turn_add(j, xs2[:, cols(j)], False, True, ident2)
+
+        def turn_back(j):
             dt = sb.tile([P, BANK], F32, name=f"dt{j}")
             nc.scalar.copy(out=dt[:], in_=st1[j][:])
-            bk = ps.tile([P, BANK], F32, name=f"bk{j}", tag=f"pt{j}")
+            bk = ps.tile([P, BANK], F32, name=f"bk{j}", tag=f"bank{(4, 5, 6, 3)[j]}")
             for k in range(4):
                 blk = slice(k * P, (k + 1) * P)
                 nc.tensor.transpose(bk[:, blk], dt[:, blk], ident[:])
-            back.append(bk[:])
-        for j in range(VEC_BANKS):
-            part = sb.tile([P, BANK], F32, name=f"part{j}")
-            nc.vector.tensor_tensor(out=part[:], in0=back[j], in1=xs2[:, cols(j)], op=add)
-            back[j] = part[:]
+            return bk[:]
+
+        a1 = [sb.tile([P, BANK], F32, name=f"a1_{j}") for j in range(NB)]
+        for j in range(NB):
+            scaled(a1[j][:], p[:, cols(j)], c0[:])
+            turn_add(j, a1[j][:], False, j == 0)
+            if j == 0:
+                scaled(v2[:], px2[:], c2[:])
+                nc.vector.tensor_tensor(out=xs1[:].indirect(o2[:]), in0=v2[:], in1=w2, op=add)
+            if j == 1:
+                first = turn_back(0)
+        part = sb.tile([P, BANK], F32, name="part")
+        nc.vector.tensor_tensor(out=part[:], in0=first, in1=xs2[:, cols(0)], op=add)
+        back = [part[:]]
+        ident2 = sb.tile([P, P], F32, name="ident2", tag="p")
+        nc.scalar.copy(out=ident2[:], in_=ident[:])
+        for j in range(1, NB):
+            turn_add(j, xs2[:, cols(j)], False, True, ident2)
+            back.append(turn_back(j))
         pieces = [(j, 0, BANK) for j in (1, 0, 2)] + [(NB - 1, 0, BANK // 2), (NB - 1, BANK // 2, BANK)]
         for n, (j, lo, hi) in enumerate(pieces):
             res = sb.tile([P, hi - lo], F32, name=f"res{n}")

from contextlib import ExitStack

import concourse.mybir as mybir
from concourse.masks import make_identity

D, V, Q, NL = 512, 2048, 128, 512
FLOPS = 2 * 2 * D * Q * V

F32 = mybir.dt.float32
BF16 = mybir.dt.bfloat16
I32 = mybir.dt.int32
U32 = mybir.dt.uint32
U16 = mybir.dt.uint16
U8 = mybir.dt.uint8
FP8X4 = mybir.dt.float8_e4m3fn_x4
FP4X4 = mybir.dt.float4_e2m1fn_x4
ALU = mybir.AluOpType
ACT = mybir.ActivationFunctionType
AX = mybir.AxisListType

P = 128
BANK = 512
NB = V // BANK
VEC_BANKS = 1


def tile_attend_hvjointcover_heads_kernel(tc, hid, voc_words, voc_scales, stake, dhid, base, offs, offs2, out):
    nc = tc.nc
    mult, add, sub = ALU.mult, ALU.add, ALU.subtract
    with ExitStack() as ctx:
        lists = ctx.enter_context(tc.tile_pool(name="lists", bufs=1))
        sb = ctx.enter_context(tc.tile_pool(name="sb", bufs=1))
        ps = ctx.enter_context(tc.psum_pool(name="ps", bufs=1))

        def cols(j):
            return slice(j * BANK, (j + 1) * BANK)

        vsc = sb.tile([P, V], U8, name="vsc", align_bytes=64)
        nc.gpsimd.memset(vsc[:].bitcast(I32), 0)
        zero = sb.tile([P, 1], F32, name="zero")
        nc.vector.memset(zero[:], 0.0)
        one = sb.tile([P, 1], F32, name="one")
        nc.scalar.activation(out=one[:], in_=zero[:], func=ACT.Exp)

        hraw = sb.tile([P, 4, Q], F32, name="hraw", tag="in0", align_bytes=64)
        words = [sb.tile([P, V], U8, name=f"words{h}", tag=f"in{2 + h}", align_bytes=64) for h in range(2)]
        w32 = voc_words[0].bitcast(I32)
        nc.sync.dma_start(out=hraw[:], in_=hid.rearrange("(p j) q -> p j q", j=4))
        s32 = voc_scales[0].bitcast(I32)
        for g in range(4):
            nc.sync.dma_start(out=vsc[32 * g : 32 * g + 4, :].bitcast(I32), in_=s32[4 * g : 4 * g + 4, :])
        nc.sync.dma_start(out=words[0][:].bitcast(I32), in_=w32[:, :BANK])
        draw = sb.tile([P, 4, Q], F32, name="draw", tag="in1", align_bytes=64)
        nc.sync.dma_start(out=draw[:], in_=dhid.rearrange("(p j) q -> p j q", j=4))
        nc.sync.dma_start(out=words[1][:].bitcast(I32), in_=w32[:, BANK:])
        o1 = lists.tile([P, NL // 16], U16, name="o1")
        o2 = lists.tile([P, NL // 16], U16, name="o2")
        nc.sync.dma_start(o1[:], offs)
        nc.sync.dma_start(o2[:], offs2)

        xs2 = sb.tile([P, V], F32, name="xs2")
        nc.vector.memset(xs2[:], 0.0)
        ident = sb.tile([P, P], F32, name="ident")
        make_identity(nc, ident[:])

        hg = sb.tile([P, Q, 4], BF16, name="hg", tag="hg", align_bytes=64)
        dg = sb.tile([P, Q, 4], BF16, name="dg", tag="dg", align_bytes=64)
        hq = sb.tile([P, Q], U32, name="hq", align_bytes=64)
        dq = sb.tile([P, Q], U32, name="dq", align_bytes=64)
        hs = sb.tile([P, Q], U8, name="hs", align_bytes=64)
        ds = sb.tile([P, Q], U8, name="ds", align_bytes=64)
        nc.vector.tensor_copy(out=hg[:], in_=hraw[:].rearrange("p j q -> p q j"))
        nc.vector.quantize_mx(out=hq[:].bitcast(FP8X4), scales=hs[:], in_=hg[:].rearrange("p q j -> p (q j)"))
        nc.scalar.copy(out=dg[:], in_=draw[:].rearrange("p j q -> p q j"))
        nc.vector.quantize_mx(out=dq[:].bitcast(FP8X4), scales=ds[:], in_=dg[:].rearrange("p q j -> p (q j)"))

        inp = sb.tile([P, 3], F32, name="inp")
        nc.vector.memset(inp[:, 0:1], -16.0)

        def scores(codes, scales, name, where):
            banks = []
            for j in range(NB):
                b = ps.tile([P, BANK], F32, name=f"{name}{j}", tag=f"bank{where[j]}")
                wj = words[j // 2][:, (j % 2) * 2 * BANK : (j % 2 + 1) * 2 * BANK]
                nc.tensor.matmul_mx(out=b[:], lhsT=codes[:].bitcast(FP8X4), lhsT_scale=scales[:],
                                    rhs=wj.bitcast(FP4X4), rhs_scale=vsc[:, cols(j)], start=True, stop=True)
                banks.append(b)
            return banks

        pa = scores(hq, hs, "pa", (0, 1, 2, 3))
        xs1 = sb.tile([P, V], F32, name="xs1", tag="hg", align_bytes=64)
        nc.gpsimd.memset(xs1[:], 0.0)
        pt = scores(dq, ds, "pt", (4, 5, 6, 3))

        stk = sb.tile([P, 1], F32, name="stk", tag="dg", align_bytes=64)
        nc.sync.dma_start(out=stk[:], in_=stake)
        bs = [sb.tile([P, BANK], F32, name=f"bs{j}", tag=f"in{j}", align_bytes=64) for j in range(NB)]
        for j in range(NB):
            nc.sync.dma_start(out=bs[j][:], in_=base[:, cols(j)])

        def scaled(dst, src, scale):
            nc.scalar.activation(out=dst, in_=src, func=ACT.Copy, scale=scale)

        def affine(dst, src, scale, bias):
            nc.scalar.activation(out=dst, in_=src, func=ACT.Identity, scale=scale, bias=bias)

        def ts(dst, src, s1_, s2_=None, op1=None):
            if s2_ is None:
                nc.vector.tensor_scalar(out=dst, in0=src, scalar1=s1_, scalar2=None, op0=mult)
            else:
                nc.vector.tensor_scalar(out=dst, in0=src, scalar1=s1_, scalar2=s2_, op0=mult, op1=op1)

        def col(name, width=1):
            return sb.tile([P, width], F32, name=name)

        a_sb = sb.tile([P, V], F32, name="a_sb")
        t_sb = sb.tile([P, V], F32, name="t_sb")
        p = sb.tile([P, V], F32, name="p", tag="p")
        mx, zp = col("mx", NB), col("zp", 3)
        for j in range(NB):
            nc.vector.tensor_scalar(out=a_sb[:, cols(j)], in0=pa[j][:], scalar1=1.0, scalar2=None, op0=mult,
                                    op1=ALU.max, accum_out=mx[:, j : j + 1])
        negm = col("negm")
        nc.vector.tensor_reduce(out=negm[:], in_=mx[:], axis=AX.X, op=ALU.max, negate=True)
        for j in range(NB - 1):
            nc.scalar.copy(out=t_sb[:, cols(j)], in_=pt[j][:])
        nc.vector.tensor_scalar(out=inp[:, 1:2], in0=stk[:], scalar1=8192.0, scalar2=one[:], op0=mult, op1=mult)
        ts(inp[:, 2:3], stk[:], -16384.0)
        ag1 = sb.tile([P, NL], F32, name="ag1")
        ag2 = sb.tile([P, NL], F32, name="ag2")
        px1 = sb.tile([P, NL], F32, name="px1")
        px2 = sb.tile([P, NL], F32, name="px2")
        nc.vector.tensor_copy(out=ag1[:], in_=a_sb[:].indirect(o1[:]))
        nc.vector.tensor_copy(out=ag2[:], in_=a_sb[:].indirect(o2[:]))
        nc.vector.tensor_copy(out=t_sb[:, cols(NB - 1)], in_=pt[NB - 1][:])

        ss, den, rec = col("ss", 2), col("den", 4), col("rec", 4)
        s1, s2, z = ss[:, 0:1], ss[:, 1:2], den[:, 1:2]
        yy = col("yy", 8)
        qq, gg, bdn = col("qq"), col("gg", 7), col("bdn")

        def dense_exp(lo, hi, n):
            nc.scalar.activation(out=p[:, lo:hi], in_=a_sb[:, lo:hi], func=ACT.Exp, bias=negm[:], accum_out=zp[:, n : n + 1])

        sg = sb.tile([P, 1], F32, name="sg", tag="w")
        za = col("za")
        dense_exp(0, 2 * BANK, 0)
        nc.scalar.activation(out=px1[:], in_=ag1[:], func=ACT.Exp, bias=negm[:], accum_out=s1)
        dense_exp(2 * BANK, 3 * BANK, 1)
        nc.scalar.activation(out=px2[:], in_=ag2[:], func=ACT.Exp, bias=negm[:], accum_out=s2)
        scaled(yy[:, 5:8], inp[:], s1)
        affine(za[:], zp[:, 0:1], 1.0, zp[:, 1:2])
        dense_exp(3 * BANK, V, 2)
        ts(sg[:], s1, s2, 16.0, mult)
        scaled(yy[:, 0:2], inp[:, 0:2], s2)
        scaled(qq[:], yy[:, 7:8], s2)
        nc.scalar.activation(out=den[:, 2:4], in_=ss[:], func=ACT.Copy, bias=1e-30)
        affine(z, zp[:, 2:3], 1.0, za[:])
        affine(den[:, 0:1], z, z, sg[:])
        xpx1 = sb.tile([P, NL], F32, name="xpx1")
        xpx2 = sb.tile([P, NL], F32, name="xpx2")
        nc.vector.tensor_tensor(out=xpx1[:], in0=t_sb[:].indirect(o1[:]), in1=px1[:], op=mult)
        nc.vector.tensor_tensor(out=xpx2[:], in0=t_sb[:].indirect(o2[:]), in1=px2[:], op=mult)
        ts(yy[:, 2:3], inp[:, 1:2], 1.0)
        nc.vector.reciprocal(out=rec[:], in_=den[:])
        idd, r = rec[:, 0:1], rec[:, 1:2]
        ts(bdn[:], qq[:], idd, r, mult)
        scaled(yy[:, 3:4], z, z)
        scaled(yy[:, 4:5], z, -2.0)

        a2 = sb.tile([P, V], F32, name="a2")
        xzp = col("xzp", NB)
        for j in range(NB):
            nc.vector.scalar_tensor_tensor(out=a2[:, cols(j)], in0=pt[j][:], scalar=bdn[:], in1=p[:, cols(j)],
                                           op0=mult, op1=mult, accum_out=xzp[:, j : j + 1])

        ww = sb.tile([P, 2 * NL], F32, name="ww", tag="w")
        w1, w2 = ww[:, :NL], ww[:, NL:]
        tt = col("tt", 2)
        t1, t2 = tt[:, 0:1], tt[:, 1:2]
        nc.scalar.activation(out=w1, in_=xpx1[:], func=ACT.Copy, accum_out=t1)
        scaled(gg[:], yy[:, 0:7], idd)
        gs2, b1, aa, g, nz2, gs1, b2 = (gg[:, n : n + 1] for n in range(7))
        nc.scalar.activation(out=w2, in_=xpx2[:], func=ACT.Copy, accum_out=t2)
        ag, e1, e2, be12, be0, h1 = col("ag"), col("e1"), col("e2"), col("be12", 2), col("be0"), col("h1")
        agt, h2, al1, al2, al0 = col("agt", 2), col("h2"), col("al1"), col("al2"), col("al0")
        scaled(ag[:], aa, g)
        scaled(e1[:], b1, gs2)
        scaled(e2[:], b2, gs1)
        scaled(be12[:], rec[:, 2:4], g)
        affine(be0[:], r, -1.0, nz2)
        scaled(h1[:], t1, b1)
        scaled(agt[:], tt[:], ag[:])
        affine(h2[:], t2, b2, h1[:])
        scaled(w1, xpx1[:], b1)
        affine(al1[:], t1, e1[:], agt[:, 1:2])
        affine(al2[:], t2, e2[:], agt[:, 0:1])
        scaled(al0[:], h2[:], nz2)
        scaled(w2, xpx2[:], b2)

        c1, c0, c2, cj = col("c1"), col("c0"), col("c2"), col("cj", 3 * NB)
        for n, (c, be, al) in enumerate(((c1, be12[:, 0:1], al1), (c0, be0[:], al0), (c2, be12[:, 1:2], al2))):
            nc.vector.tensor_scalar(out=cj[:, n * NB : (n + 1) * NB], in0=xzp[:], scalar1=be, scalar2=al[:], op0=mult, op1=add,
                                    accum_out=c[:])
        v1 = sb.tile([P, NL], F32, name="v1")
        v2 = sb.tile([P, NL], F32, name="v2")
        ts(v1[:], px1[:], c1[:])
        nc.vector.tensor_tensor(out=xs2[:].indirect(o1[:]), in0=v1[:], in1=w1, op=add)
        st1 = [ps.tile([P, BANK], F32, name=f"st{j}", tag=f"bank{(0, 1, 2, 7)[j]}") for j in range(NB)]

        def turn_add(j, src, first, last, eye=ident):
            for k in range(4):
                blk = slice(k * P, (k + 1) * P)
                nc.tensor.matmul(st1[j][:, blk], lhsT=src[:, blk], rhs=eye[:], is_transpose=True,
                                 start=(first and k == 0), stop=(last and k == 3))

        for j in range(NB):
            turn_add(j, bs[j][:], True, False)
        for j in range(NB):
            turn_add(j, a2[:, cols(j)], False, False)

        def turn_back(j):
            dt = sb.tile([P, BANK], F32, name=f"dt{j}")
            nc.scalar.copy(out=dt[:], in_=st1[j][:])
            bk = ps.tile([P, BANK], F32, name=f"bk{j}", tag=f"bank{(4, 5, 6, 3)[j]}")
            for k in range(4):
                blk = slice(k * P, (k + 1) * P)
                nc.tensor.transpose(bk[:, blk], dt[:, blk], ident[:])
            return bk[:]

        a1 = [sb.tile([P, BANK], F32, name=f"a1_{j}") for j in range(NB)]
        for j in range(NB):
            scaled(a1[j][:], p[:, cols(j)], c0[:])
            turn_add(j, a1[j][:], False, j == 0)
            if j == 0:
                scaled(v2[:], px2[:], c2[:])
                nc.vector.tensor_tensor(out=xs1[:].indirect(o2[:]), in0=v2[:], in1=w2, op=add)
            if j == 1:
                first = turn_back(0)
        part = sb.tile([P, BANK], F32, name="part")
        nc.vector.tensor_tensor(out=part[:], in0=first, in1=xs2[:, cols(0)], op=add)
        back = [part[:]]
        ident2 = sb.tile([P, P], F32, name="ident2", tag="p")
        nc.scalar.copy(out=ident2[:], in_=ident[:])
        for j in range(1, NB):
            turn_add(j, xs2[:, cols(j)], False, True, ident2)
            back.append(turn_back(j))
        pieces = [(j, 0, BANK) for j in (1, 0, 2)] + [(NB - 1, 0, BANK // 2), (NB - 1, BANK // 2, BANK)]
        for n, (j, lo, hi) in enumerate(pieces):
            res = sb.tile([P, hi - lo], F32, name=f"res{n}")
            span = slice(j * BANK + lo, j * BANK + hi)
            nc.vector.tensor_tensor(out=res[:], in0=back[j][:, lo:hi], in1=xs1[:, span], op=add)
            nc.sync.dma_start(out=out[:, span], in_=res[:])
